import numpy as np
import ml_dtypes


def mxq(x, axis, fmt="e4m3"):
    dtype, down = {"e4m3": (ml_dtypes.float8_e4m3fn, 7), "e5m2": (ml_dtypes.float8_e5m2, 14)}[fmt]
    v = np.moveaxis(np.asarray(x, np.float32).astype(ml_dtypes.bfloat16).astype(np.float64), axis, -1)
    blocks = v.reshape(v.shape[:-1] + (-1, 32))
    amax = np.abs(blocks).max(-1, keepdims=True)
    byte = np.maximum(np.where(amax > 0, np.frexp(amax)[1] - 1 + 127, 0) - down, 1)
    scale = np.exp2(byte - 127.0)
    codes = (blocks / scale).astype(np.float32).astype(dtype).astype(np.float64)
    return np.moveaxis((codes * scale).reshape(v.shape), -1, axis)


WIDE = False


def mx_kscale(k):
    if not WIDE:
        return np.ones(k)
    levels = np.array([10, -10, 5, -5, 0])
    if k % 512:
        return np.exp2(np.random.permutation(np.resize(levels, k // 32))).repeat(32)
    a = np.empty((k // 512, 16))
    for p in range(k // 512):
        a[p, :8] = np.random.permutation(np.resize(levels, 8))
        for g in range(8):
            far = levels[np.abs(levels - a[p, g]) >= 10]
            a[p, g + 8] = far[np.random.randint(len(far))]
    return np.exp2(a.ravel()).repeat(32)


BF16 = ml_dtypes.bfloat16


def bf(x):
    return np.asarray(x, np.float32).astype(BF16)


def f64(x):
    return np.asarray(x).astype(np.float64)


E2M1 = np.array([0.0, 0.5, 1.0, 1.5, 2.0, 3.0, 4.0, 6.0, -0.0, -0.5, -1.0, -1.5, -2.0, -3.0, -4.0, -6.0])


def pack_weight(w, fmt):
    k, n = w.shape
    w = f64(bf(w)).reshape(k // 32, 32, n)
    amax = np.abs(w).max(1)
    if fmt == "e4m3":
        byte = np.frexp(amax)[1] - 1 + 127 - 7
    else:
        mant, ex = np.frexp(amax / 6.0)
        byte = np.where(mant > 0.5, ex, ex - 1) + 127
    byte = np.clip(np.where(amax > 0, byte, 1), 1, 254)
    scaled = (w * np.exp2(127.0 - byte)[:, None, :]).reshape(k, n).astype(np.float32)
    by_word = np.ascontiguousarray(scaled.reshape(k // 512, 128, 4, n).transpose(0, 1, 3, 2))
    if fmt == "e4m3":
        words = by_word.astype(ml_dtypes.float8_e4m3fn).view(np.uint8)
    else:
        c = by_word.astype(ml_dtypes.float4_e2m1fn).view(np.uint8) & 0xF
        words = c[..., 0::2] | (c[..., 1::2] << 4)
    return np.ascontiguousarray(words), np.ascontiguousarray(byte.astype(np.uint8).reshape(k // 512, 16, n))


def unpack_weight(words, scales, fmt):
    g, p, n, _ = words.shape
    if fmt == "e4m3":
        vals = np.ascontiguousarray(words).view(ml_dtypes.float8_e4m3fn).astype(np.float64)
    else:
        nib = np.empty((g, p, n, 4), np.uint8)
        nib[..., 0::2] = words & 0xF
        nib[..., 1::2] = words >> 4
        vals = E2M1[nib]
    vals = vals * np.repeat(np.exp2(scales.astype(np.float64) - 127.0), 8, axis=1)[..., None]
    return vals.transpose(0, 1, 3, 2).reshape(g * 512, n)
def pack4(w):
    words, scales = pack_weight(w, "e2m1")
    return words.reshape(words.shape[0], 128, -1), scales


def unpack4(words, scales):
    return unpack_weight(words.reshape(words.shape[0], 128, -1, 2), scales, "e2m1")


M, K, J, C = 1024, 1536, 2048, 512


def setup_inputs():
    s = mx_kscale(K)
    t = mx_kscale(J)
    u_words, u_scales = pack4(np.random.standard_normal((K, M)) * s[:, None])
    v_words, v_scales = pack4(np.random.standard_normal((K, J)) / np.sqrt(K) / s[:, None])
    r = np.random.uniform(0.8, 1.6, (M, J))
    return {"u_words": u_words, "u_scales": u_scales,
            "v_words": v_words, "v_scales": v_scales,
            "dist": bf(r ** -6.0 * t),
            "pop": bf(np.random.standard_normal((J, C)) / np.sqrt(J) / t[:, None]),
            "acc": bf(np.random.standard_normal((M, C))),
            "decay": bf(np.random.uniform(0.5, 1.5, M))}


def reference(u_words, u_scales, v_words, v_scales, dist, pop, acc, decay):
    u = unpack4(u_words, u_scales)
    v = unpack4(v_words, v_scales)
    g = u.T @ v
    rate = np.square(g) * f64(dist)
    gain = mxq(rate, 1, "e4m3") @ mxq(f64(pop), 0, "e4m3")
    return gain - f64(decay)[:, None] * f64(acc)

@@ -1,0 +1,255 @@
+from contextlib import ExitStack
+
+import concourse.mybir as mybir
+from concourse.masks import make_identity
+
+M, K, J, C = 1024, 1536, 2048, 512
+FLOPS = 2 * M * K * J + 2 * M * J * C
+
+F32 = mybir.dt.float32
+BF16 = mybir.dt.bfloat16
+I32 = mybir.dt.int32
+U32 = mybir.dt.uint32
+U8 = mybir.dt.uint8
+FP4X4 = mybir.dt.float4_e2m1fn_x4
+FP8X4 = mybir.dt.float8_e4m3fn_x4
+ACT = mybir.ActivationFunctionType
+ALU = mybir.AluOpType
+
+P = 128
+BANK = 512
+K_PASSES = K // 512
+J_PASSES = J // 512
+M_TILES = M // P
+U_FIRST = 2
+GAIN_LAG = 4
+ALIGN = 64
+
+
+def tile_forster_like_energy_transfer_s4_kernel(
+    tc, u_words, u_scales, v_words, v_scales, dist, pop, acc, decay, out
+):
+    nc = tc.nc
+    with ExitStack() as ctx:
+        keep = ctx.enter_context(tc.tile_pool(name="keep", bufs=1))
+        work = ctx.enter_context(tc.tile_pool(name="work", bufs=4))
+        psum = ctx.enter_context(tc.psum_pool(name="psum", bufs=1))
+        ctx.enter_context(tc.manual_schedule())
+
+        def kept(shape, dtype, name):
+            return keep.tile(shape, dtype, name=name, align_bytes=ALIGN)
+
+        def bank(tag):
+            return psum.tile([P, BANK], F32, name=tag, tag=tag)
+
+        def load_codes(words, first, count, name):
+            codes = kept([P, K_PASSES, 2 * count], U8, name)
+            src = words.bitcast(I32).rearrange("g p w -> p g w")
+            nc.sync.dma_start(out=codes[:].bitcast(I32), in_=src[:, :, first // 2 : (first + count) // 2])
+            return codes
+
+        def scale_plane(count, name):
+            plane = kept([P, K_PASSES, count], U8, name)
+            nc.vector.memset(plane[:].bitcast(I32), 0)
+            return plane
+
+        def load_scale_rows(plane, scales, first, rows):
+            count = plane.shape[2]
+            src = scales.bitcast(I32).rearrange("g (q r) w -> r q g w", r=4)
+            for r in rows:
+                nc.sync.dma_start(
+                    out=plane[r:P:32].bitcast(I32), in_=src[r, :, :, first // 4 : (first + count) // 4]
+                )
+
+        def load_dist(i):
+            rows = kept([P, J], BF16, "dist%d" % i)
+            nc.sync.dma_start(out=rows[:], in_=dist[i * P : (i + 1) * P, :])
+            return rows
+
+        def load_pop(g):
+            raw = kept([P, 4, C], BF16, "pop_raw%d" % g)
+            nc.sync.dma_start(out=raw[:], in_=pop[512 * g : 512 * (g + 1), :].rearrange("(p t) c -> p t c", t=4))
+            return raw
+
+        m_first = U_FIRST * P
+        u_plane = [scale_plane(m_first, "us0")]
+        v_plane = [scale_plane(J // 2, "vs0"), scale_plane(J // 2, "vs1")]
+        u_plane.append(scale_plane(M - m_first, "us1"))
+        decay_rows = kept([P, P], F32, "decay_rows")
+        nc.vector.memset(decay_rows[:], 0.0)
+
+        ident_bf = kept([P, P], BF16, "ident_bf")
+        make_identity(nc, ident_bf[:])
+        ident = kept([P, P], F32, "ident")
+        nc.scalar.activation(out=ident[:], in_=ident_bf[:], func=ACT.Square)
+
+        load_scale_rows(u_plane[0], u_scales, 0, (0, 1))
+        v_codes = [load_codes(v_words, 0, BANK, "vc0")]
+        u_codes = [load_codes(u_words, 0, m_first, "uc0")]
+        load_scale_rows(u_plane[0], u_scales, 0, (2, 3))
+        load_scale_rows(v_plane[0], v_scales, 0, range(4))
+        v_codes.append(load_codes(v_words, BANK, BANK, "vc1"))
+        load_scale_rows(v_plane[1], v_scales, J // 2, range(4))
+        v_codes.append(load_codes(v_words, 2 * BANK, BANK, "vc2"))
+        v_codes.append(load_codes(v_words, 3 * BANK, BANK, "vc3"))
+        pop_raw = [load_pop(0)]
+        dist_rows = [load_dist(0)]
+        u_codes.append(load_codes(u_words, m_first, M - m_first, "uc1"))
+        load_scale_rows(u_plane[1], u_scales, m_first, range(4))
+        dist_rows.append(load_dist(1))
+        pop_raw.append(load_pop(1))
+        decay_raw = kept([M_TILES, P], BF16, "decay_raw")
+        nc.sync.dma_start(out=decay_raw[:], in_=decay.rearrange("(i p) -> i p", p=P))
+        dist_rows.append(load_dist(2))
+        pop_raw.append(load_pop(2))
+        pop_raw.append(load_pop(3))
+        dist_rows.append(load_dist(3))
+        acc_rows = []
+        for half in range(2):
+            rows = kept([P, M_TILES // 2, C], BF16, "acc%d" % half)
+            src = acc[half * M // 2 : (half + 1) * M // 2, :]
+            nc.sync.dma_start(out=rows[:], in_=src.rearrange("(i p) c -> p i c", p=P))
+            acc_rows.append(rows)
+            dist_rows.append(load_dist(4 + half))
+        dist_rows.append(load_dist(6))
+        dist_rows.append(load_dist(7))
+
+        pop_grouped, pop_codes, pop_scales = {}, {}, {}
+        squares, rates, rate_grouped, rate_codes, rate_scales = {}, {}, {}, {}, {}
+        neg_decay = kept([P, M_TILES], F32, "neg_decay")
+
+        def interleave_pop(g):
+            grouped = kept([P, C, 4], BF16, "pop_grouped%d" % g)
+            nc.vector.tensor_copy(
+                out=grouped[:].rearrange("p (c i) t -> p c t i", i=4),
+                in_=pop_raw[g][:].rearrange("p t (c i) -> p c t i", i=4),
+            )
+            pop_grouped[g] = grouped
+
+        def quantize_pop(g):
+            pop_codes[g] = kept([P, C], U32, "pop_codes%d" % g)
+            pop_scales[g] = kept([P, C], U8, "pop_scales%d" % g)
+            nc.vector.quantize_mx(
+                out=pop_codes[g][:].bitcast(FP8X4),
+                scales=pop_scales[g][:],
+                in_=pop_grouped[g][:].rearrange("p c t -> p (c t)"),
+            )
+
+        def inner_products(i, g):
+            part, col = (0, i * P) if i < U_FIRST else (1, i * P - m_first)
+            products = bank("g%d" % g)
+            v_col = (g % 2) * BANK
+            for k in range(K_PASSES):
+                nc.tensor.matmul_mx(
+                    out=products[:],
+                    lhsT=u_codes[part][:, k, 2 * col : 2 * (col + P)].bitcast(FP4X4),
+                    lhsT_scale=u_plane[part][:, k, col : col + P],
+                    rhs=v_codes[g][:, k, :].bitcast(FP4X4),
+                    rhs_scale=v_plane[g // 2][:, k, v_col : v_col + BANK],
+                    start=(k == 0),
+                    stop=(k == K_PASSES - 1),
+                )
+            if g % 2 == 0:
+                squares[i, g // 2] = work.tile([P, 2, 2, 256], F32, name="square")
+            nc.scalar.activation(
+                out=squares[i, g // 2][:, :, g % 2, :].rearrange("p u (q e) -> p u q e", e=2),
+                in_=products[:].rearrange("p (q u e) -> p u q e", u=2, e=2),
+                func=ACT.Square,
+            )
+
+        def multiply_dist(i, h):
+            rate = work.tile([P, 2, 256, 2], BF16, name="rate", align_bytes=ALIGN)
+            nc.vector.tensor_tensor(
+                out=rate[:],
+                in0=squares[i, h][:].rearrange("p u g (q e) -> p u (g q) e", e=2),
+                in1=dist_rows[i][:, 1024 * h : 1024 * (h + 1)].rearrange("p (q u e) -> p u q e", u=2, e=2),
+                op=ALU.mult,
+            )
+            rates[i, h] = rate
+
+        def turn_rate(i, h):
+            words = rates[i, h][:].rearrange("p u q e -> p (u q e)").bitcast(F32)
+            turned = bank("t%d" % h)
+            for g in range(2):
+                for u in range(2):
+                    src = 256 * u + P * g
+                    dst = 256 * g + P * u
+                    nc.tensor.transpose(turned[:, dst : dst + P], words[:, src : src + P], ident[:])
+            grouped = work.tile([P, 1024], BF16, name="rate_grouped", align_bytes=ALIGN)
+            nc.scalar.copy(
+                out=grouped[:].bitcast(F32).rearrange("p (g m u) -> p g m u", g=2, u=2),
+                in_=turned[:].rearrange("p (g u m) -> p g m u", g=2, u=2),
+            )
+            rate_grouped[i, h] = grouped
+
+        def quantize_rate(i, h):
+            rate_codes[i, h] = kept([P, 256], U32, "rate_codes%d_%d" % (i, h))
+            rate_scales[i, h] = kept([P, 256], U8, "rate_scales%d_%d" % (i, h))
+            nc.vector.quantize_mx(
+                out=rate_codes[i, h][:].bitcast(FP8X4), scales=rate_scales[i, h][:], in_=rate_grouped[i, h][:]
+            )
+
+        def turn_decay():
+            turned = bank("o1")
+            nc.tensor.transpose(turned[:, 0:P], decay_rows[:], ident[:])
+            nc.scalar.copy(out=neg_decay[:], in_=turned[:, 0:M_TILES])
+
+        def gain(i, tag, c0, width):
+            sums = bank(tag)
+            for g in range(J_PASSES):
+                cols = slice((g % 2) * P, (g % 2 + 1) * P)
+                nc.tensor.matmul_mx(
+                    out=sums[:, 0:width],
+                    lhsT=rate_codes[i, g // 2][:, cols].bitcast(FP8X4),
+                    lhsT_scale=rate_scales[i, g // 2][:, cols],
+                    rhs=pop_codes[g][:, c0 : c0 + width].bitcast(FP8X4),
+                    rhs_scale=pop_scales[g][:, c0 : c0 + width],
+                    start=(g == 0),
+                    stop=(g == J_PASSES - 1),
+                )
+            result = kept([P, width], F32, "result%d_%d" % (i, c0))
+            nc.vector.scalar_tensor_tensor(
+                out=result[:],
+                in0=acc_rows[i // 4][:, i % 4, c0 : c0 + width],
+                scalar=neg_decay[:, i : i + 1],
+                in1=sums[:, 0:width],
+                op0=ALU.mult,
+                op1=ALU.add,
+            )
+            nc.sync.dma_start(out=out[i * P : (i + 1) * P, c0 : c0 + width], in_=result[:])
+
+        interleave_pop(0)
+        for i in range(M_TILES):
+            inner_products(i, 0)
+            inner_products(i, 1)
+            if i == 2:
+                nc.vector.tensor_scalar_mul(out=decay_rows[0:M_TILES, :], in0=decay_raw[:], scalar1=-1.0)
+            multiply_dist(i, 0)
+            if i == 0:
+                quantize_pop(0)
+            elif i < J_PASSES:
+                interleave_pop(i)
+            inner_products(i, 2)
+            inner_products(i, 3)
+            multiply_dist(i, 1)
+            if 0 < i < J_PASSES:
+                quantize_pop(i)
+            if i > 0:
+                turn_rate(i - 1, 0)
+                turn_rate(i - 1, 1)
+                if i == 2:
+                    turn_decay()
+                quantize_rate(i - 1, 0)
+                quantize_rate(i - 1, 1)
+            if i >= GAIN_LAG:
+                gain(i - GAIN_LAG, "o%d" % (i % 2), 0, C)
+        last = M_TILES - 1
+        gain(4, "o0", 0, C)
+        turn_rate(last, 0)
+        turn_rate(last, 1)
+        quantize_rate(last, 0)
+        quantize_rate(last, 1)
+        gain(5, "o1", 0, C)
+        gain(6, "g0", 0, C)
+        gain(last, "g1", 0, C // 2)
+        gain(last, "g2", C // 2, C // 2)

@@ -21,8 +21,7 @@ BANK = 512
 K_PASSES = K // 512
 J_PASSES = J // 512
 M_TILES = M // P
-U_FIRST = 2
-GAIN_LAG = 4
+PAIRS = M_TILES // 2
 ALIGN = 64
 
 
@@ -41,6 +40,12 @@ def tile_forster_like_energy_transfer_s4_kernel(
 
         def bank(tag):
             return psum.tile([P, BANK], F32, name=tag, tag=tag)
+
+        sum_banks_taken = []
+
+        def sum_bank():
+            sum_banks_taken.append(None)
+            return bank("sums%d" % (len(sum_banks_taken) % 4))
 
         def load_codes(words, first, count, name):
             codes = kept([P, K_PASSES, 2 * count], U8, name)
@@ -61,9 +66,16 @@ def tile_forster_like_energy_transfer_s4_kernel(
                     out=plane[r:P:32].bitcast(I32), in_=src[r, :, :, first // 4 : (first + count) // 4]
                 )
 
-        def load_dist(i):
-            rows = kept([P, J], BF16, "dist%d" % i)
-            nc.sync.dma_start(out=rows[:], in_=dist[i * P : (i + 1) * P, :])
+        def load_dist(pair, h):
+            rows = kept([P, 2, J // 2], BF16, "dist%d_%d" % (pair, h))
+            src = dist[2 * P * pair : 2 * P * (pair + 1), h * J // 2 : (h + 1) * J // 2]
+            nc.sync.dma_start(out=rows[:], in_=src.rearrange("(s p) j -> p s j", p=P))
+            dist_rows[pair, h] = rows
+
+        def load_acc(half):
+            rows = kept([P, M_TILES // 2, C], BF16, "acc%d" % half)
+            src = acc[half * M // 2 : (half + 1) * M // 2, :]
+            nc.sync.dma_start(out=rows[:], in_=src.rearrange("(i p) c -> p i c", p=P))
             return rows
 
         def load_pop(g):
@@ -71,60 +83,59 @@ def tile_forster_like_energy_transfer_s4_kernel(
             nc.sync.dma_start(out=raw[:], in_=pop[512 * g : 512 * (g + 1), :].rearrange("(p t) c -> p t c", t=4))
             return raw
 
-        m_first = U_FIRST * P
-        u_plane = [scale_plane(m_first, "us0")]
+        m_pair = 2 * P
+        u_plane = [scale_plane(m_pair, "us0")]
         v_plane = [scale_plane(J // 2, "vs0"), scale_plane(J // 2, "vs1")]
-        u_plane.append(scale_plane(M - m_first, "us1"))
+        u_plane.append(scale_plane(M - m_pair, "us1"))
+        ident_bf = kept([P, P], BF16, "ident_bf")
+        nc.vector.memset(ident_bf[:], 0.0)
+        make_identity(nc, ident_bf[:], nomemset=True)
+        ident = kept([P, P], F32, "ident")
+        nc.scalar.activation(out=ident[:], in_=ident_bf[:], func=ACT.Square)
         decay_rows = kept([P, P], F32, "decay_rows")
         nc.vector.memset(decay_rows[:], 0.0)
 
-        ident_bf = kept([P, P], BF16, "ident_bf")
-        make_identity(nc, ident_bf[:])
-        ident = kept([P, P], F32, "ident")
-        nc.scalar.activation(out=ident[:], in_=ident_bf[:], func=ACT.Square)
-
+        dist_rows = {}
         load_scale_rows(u_plane[0], u_scales, 0, (0, 1))
         v_codes = [load_codes(v_words, 0, BANK, "vc0")]
-        u_codes = [load_codes(u_words, 0, m_first, "uc0")]
+        u_codes = [load_codes(u_words, 0, m_pair, "uc0")]
         load_scale_rows(u_plane[0], u_scales, 0, (2, 3))
         load_scale_rows(v_plane[0], v_scales, 0, range(4))
         v_codes.append(load_codes(v_words, BANK, BANK, "vc1"))
         load_scale_rows(v_plane[1], v_scales, J // 2, range(4))
         v_codes.append(load_codes(v_words, 2 * BANK, BANK, "vc2"))
+        load_dist(0, 0)
         v_codes.append(load_codes(v_words, 3 * BANK, BANK, "vc3"))
+        u_codes.append(load_codes(u_words, m_pair, m_pair, "uc1"))
+        load_scale_rows(u_plane[1], u_scales, m_pair, range(4))
         pop_raw = [load_pop(0)]
-        dist_rows = [load_dist(0)]
-        u_codes.append(load_codes(u_words, m_first, M - m_first, "uc1"))
-        load_scale_rows(u_plane[1], u_scales, m_first, range(4))
-        dist_rows.append(load_dist(1))
+        load_dist(0, 1)
         pop_raw.append(load_pop(1))
+        load_dist(1, 0)
+        pop_raw.append(load_pop(2))
+        u_codes.append(load_codes(u_words, 2 * m_pair, 2 * m_pair, "uc2"))
+        load_dist(1, 1)
+        pop_raw.append(load_pop(3))
         decay_raw = kept([M_TILES, P], BF16, "decay_raw")
         nc.sync.dma_start(out=decay_raw[:], in_=decay.rearrange("(i p) -> i p", p=P))
-        dist_rows.append(load_dist(2))
-        pop_raw.append(load_pop(2))
-        pop_raw.append(load_pop(3))
-        dist_rows.append(load_dist(3))
-        acc_rows = []
-        for half in range(2):
-            rows = kept([P, M_TILES // 2, C], BF16, "acc%d" % half)
-            src = acc[half * M // 2 : (half + 1) * M // 2, :]
-            nc.sync.dma_start(out=rows[:], in_=src.rearrange("(i p) c -> p i c", p=P))
-            acc_rows.append(rows)
-            dist_rows.append(load_dist(4 + half))
-        dist_rows.append(load_dist(6))
-        dist_rows.append(load_dist(7))
+        load_dist(2, 0)
+        acc_rows = [load_acc(0)]
+        load_dist(2, 1)
+        load_dist(3, 0)
+        load_dist(3, 1)
+        acc_rows.append(load_acc(1))
 
         pop_grouped, pop_codes, pop_scales = {}, {}, {}
         squares, rates, rate_grouped, rate_codes, rate_scales = {}, {}, {}, {}, {}
         neg_decay = kept([P, M_TILES], F32, "neg_decay")
 
-        def interleave_pop(g):
-            grouped = kept([P, C, 4], BF16, "pop_grouped%d" % g)
-            nc.vector.tensor_copy(
-                out=grouped[:].rearrange("p (c i) t -> p c t i", i=4),
-                in_=pop_raw[g][:].rearrange("p t (c i) -> p c t i", i=4),
+        def interleave_pop(g, copy, c0, c1):
+            if g not in pop_grouped:
+                pop_grouped[g] = kept([P, C, 4], BF16, "pop_grouped%d" % g)
+            copy(
+                out=pop_grouped[g][:, c0:c1, :].rearrange("p (c i) t -> p c t i", i=4),
+                in_=pop_raw[g][:, :, c0:c1].rearrange("p t (c i) -> p c t i", i=4),
             )
-            pop_grouped[g] = grouped
 
         def quantize_pop(g):
             pop_codes[g] = kept([P, C], U32, "pop_codes%d" % g)
@@ -136,21 +147,24 @@ def tile_forster_like_energy_transfer_s4_kernel(
             )
 
         def inner_products(i, g):
-            part, col = (0, i * P) if i < U_FIRST else (1, i * P - m_first)
-            products = bank("g%d" % g)
+            part = min(i // 2, 2)
+            col = i * P - part * m_pair
+            s_part = min(i // 2, 1)
+            s_col = i * P - s_part * m_pair
+            products = sum_bank()
             v_col = (g % 2) * BANK
             for k in range(K_PASSES):
                 nc.tensor.matmul_mx(
                     out=products[:],
                     lhsT=u_codes[part][:, k, 2 * col : 2 * (col + P)].bitcast(FP4X4),
-                    lhsT_scale=u_plane[part][:, k, col : col + P],
+                    lhsT_scale=u_plane[s_part][:, k, s_col : s_col + P],
                     rhs=v_codes[g][:, k, :].bitcast(FP4X4),
                     rhs_scale=v_plane[g // 2][:, k, v_col : v_col + BANK],
                     start=(k == 0),
                     stop=(k == K_PASSES - 1),
                 )
             if g % 2 == 0:
-                squares[i, g // 2] = work.tile([P, 2, 2, 256], F32, name="square")
+                squares[i, g // 2] = work.tile([P, 2, 2, 256], F32, name="square", bufs=8)
             nc.scalar.activation(
                 out=squares[i, g // 2][:, :, g % 2, :].rearrange("p u (q e) -> p u q e", e=2),
                 in_=products[:].rearrange("p (q u e) -> p u q e", u=2, e=2),
@@ -158,50 +172,48 @@ def tile_forster_like_energy_transfer_s4_kernel(
             )
 
         def multiply_dist(i, h):
-            rate = work.tile([P, 2, 256, 2], BF16, name="rate", align_bytes=ALIGN)
+            rate = work.tile([P, 2, 256, 2], BF16, name="rate", bufs=8, align_bytes=ALIGN)
             nc.vector.tensor_tensor(
                 out=rate[:],
                 in0=squares[i, h][:].rearrange("p u g (q e) -> p u (g q) e", e=2),
-                in1=dist_rows[i][:, 1024 * h : 1024 * (h + 1)].rearrange("p (q u e) -> p u q e", u=2, e=2),
+                in1=dist_rows[i // 2, h][:, i % 2, :].rearrange("p (q u e) -> p u q e", u=2, e=2),
                 op=ALU.mult,
             )
             rates[i, h] = rate
 
         def turn_rate(i, h):
             words = rates[i, h][:].rearrange("p u q e -> p (u q e)").bitcast(F32)
-            turned = bank("t%d" % h)
+            turned = bank("turned%d" % (2 * (i % 2) + h))
             for g in range(2):
                 for u in range(2):
                     src = 256 * u + P * g
                     dst = 256 * g + P * u
                     nc.tensor.transpose(turned[:, dst : dst + P], words[:, src : src + P], ident[:])
-            grouped = work.tile([P, 1024], BF16, name="rate_grouped", align_bytes=ALIGN)
+            if h == 0:
+                rate_grouped[i] = work.tile([P, J], BF16, name="rate_grouped", align_bytes=ALIGN)
             nc.scalar.copy(
-                out=grouped[:].bitcast(F32).rearrange("p (g m u) -> p g m u", g=2, u=2),
+                out=rate_grouped[i][:, 1024 * h : 1024 * (h + 1)].bitcast(F32).rearrange("p (g m u) -> p g m u", g=2, u=2),
                 in_=turned[:].rearrange("p (g u m) -> p g m u", g=2, u=2),
             )
-            rate_grouped[i, h] = grouped
 
-        def quantize_rate(i, h):
-            rate_codes[i, h] = kept([P, 256], U32, "rate_codes%d_%d" % (i, h))
-            rate_scales[i, h] = kept([P, 256], U8, "rate_scales%d_%d" % (i, h))
-            nc.vector.quantize_mx(
-                out=rate_codes[i, h][:].bitcast(FP8X4), scales=rate_scales[i, h][:], in_=rate_grouped[i, h][:]
-            )
+        def quantize_rate(i):
+            rate_codes[i] = kept([P, BANK], U32, "rate_codes%d" % i)
+            rate_scales[i] = kept([P, BANK], U8, "rate_scales%d" % i)
+            nc.vector.quantize_mx(out=rate_codes[i][:].bitcast(FP8X4), scales=rate_scales[i][:], in_=rate_grouped[i][:])
 
         def turn_decay():
-            turned = bank("o1")
+            turned = sum_bank()
             nc.tensor.transpose(turned[:, 0:P], decay_rows[:], ident[:])
             nc.scalar.copy(out=neg_decay[:], in_=turned[:, 0:M_TILES])
 
-        def gain(i, tag, c0, width):
-            sums = bank(tag)
+        def gain(i, c0, width):
+            sums = sum_bank()
             for g in range(J_PASSES):
-                cols = slice((g % 2) * P, (g % 2 + 1) * P)
+                cols = slice(g * P, (g + 1) * P)
                 nc.tensor.matmul_mx(
                     out=sums[:, 0:width],
-                    lhsT=rate_codes[i, g // 2][:, cols].bitcast(FP8X4),
-                    lhsT_scale=rate_scales[i, g // 2][:, cols],
+                    lhsT=rate_codes[i][:, cols].bitcast(FP8X4),
+                    lhsT_scale=rate_scales[i][:, cols],
                     rhs=pop_codes[g][:, c0 : c0 + width].bitcast(FP8X4),
                     rhs_scale=pop_scales[g][:, c0 : c0 + width],
                     start=(g == 0),
@@ -218,38 +230,38 @@ def tile_forster_like_energy_transfer_s4_kernel(
             )
             nc.sync.dma_start(out=out[i * P : (i + 1) * P, c0 : c0 + width], in_=result[:])
 
-        interleave_pop(0)
-        for i in range(M_TILES):
-            inner_products(i, 0)
-            inner_products(i, 1)
-            if i == 2:
-                nc.vector.tensor_scalar_mul(out=decay_rows[0:M_TILES, :], in0=decay_raw[:], scalar1=-1.0)
-            multiply_dist(i, 0)
-            if i == 0:
-                quantize_pop(0)
-            elif i < J_PASSES:
-                interleave_pop(i)
-            inner_products(i, 2)
-            inner_products(i, 3)
-            multiply_dist(i, 1)
-            if 0 < i < J_PASSES:
-                quantize_pop(i)
-            if i > 0:
-                turn_rate(i - 1, 0)
-                turn_rate(i - 1, 1)
-                if i == 2:
-                    turn_decay()
-                quantize_rate(i - 1, 0)
-                quantize_rate(i - 1, 1)
-            if i >= GAIN_LAG:
-                gain(i - GAIN_LAG, "o%d" % (i % 2), 0, C)
-        last = M_TILES - 1
-        gain(4, "o0", 0, C)
-        turn_rate(last, 0)
-        turn_rate(last, 1)
-        quantize_rate(last, 0)
-        quantize_rate(last, 1)
-        gain(5, "o1", 0, C)
-        gain(6, "g0", 0, C)
-        gain(last, "g1", 0, C // 2)
-        gain(last, "g2", C // 2, C // 2)
+        def turn_pair(pair):
+            for i in (2 * pair, 2 * pair + 1):
+                turn_rate(i, 0)
+                turn_rate(i, 1)
+            if pair == 1:
+                turn_decay()
+            for i in (2 * pair, 2 * pair + 1):
+                quantize_rate(i)
+                if pair > 0:
+                    gain(i - 2, 0, C)
+
+        shared = (0, 1, 3)
+        for pair in range(PAIRS):
+            for h in range(2):
+                n = 2 * pair + h
+                inner_products(2 * pair, 2 * h)
+                inner_products(2 * pair + 1, 2 * h)
+                inner_products(2 * pair, 2 * h + 1)
+                multiply_dist(2 * pair, h)
+                inner_products(2 * pair + 1, 2 * h + 1)
+                if n - 1 in shared:
+                    interleave_pop(n - 1, nc.scalar.copy, C // 2, C)
+                multiply_dist(2 * pair + 1, h)
+                if 0 <= n - 1 < J_PASSES:
+                    quantize_pop(n - 1)
+                if n < J_PASSES:
+                    interleave_pop(n, nc.vector.tensor_copy, 0, C // 2 if n in shared else C)
+                if n == J_PASSES:
+                    nc.vector.tensor_scalar_mul(out=decay_rows[0:M_TILES, :], in0=decay_raw[:], scalar1=-1.0)
+            if pair > 0:
+                turn_pair(pair - 1)
+        turn_pair(PAIRS - 1)
+        gain(M_TILES - 2, 0, C)
+        gain(M_TILES - 1, 0, C // 2)
+        gain(M_TILES - 1, C // 2, C // 2)

@@ -104,26 +104,25 @@ def tile_forster_like_energy_transfer_s4_kernel(
         v_codes.append(load_codes(v_words, BANK, BANK, "vc1"))
         load_scale_rows(v_plane[1], v_scales, J // 2, range(4))
         v_codes.append(load_codes(v_words, 2 * BANK, BANK, "vc2"))
-        load_dist(0, 0)
         v_codes.append(load_codes(v_words, 3 * BANK, BANK, "vc3"))
+        load_dist(0, 0)
         u_codes.append(load_codes(u_words, m_pair, m_pair, "uc1"))
         load_scale_rows(u_plane[1], u_scales, m_pair, range(4))
-        pop_raw = [load_pop(0)]
         load_dist(0, 1)
-        pop_raw.append(load_pop(1))
+        pop_raw = [load_pop(0)]
         load_dist(1, 0)
-        pop_raw.append(load_pop(2))
         u_codes.append(load_codes(u_words, 2 * m_pair, 2 * m_pair, "uc2"))
         load_dist(1, 1)
-        pop_raw.append(load_pop(3))
+        pop_raw.append(load_pop(1))
         decay_raw = kept([M_TILES, P], BF16, "decay_raw")
         nc.sync.dma_start(out=decay_raw[:], in_=decay.rearrange("(i p) -> i p", p=P))
         load_dist(2, 0)
-        acc_rows = [load_acc(0)]
+        pop_raw.append(load_pop(2))
         load_dist(2, 1)
+        pop_raw.append(load_pop(3))
         load_dist(3, 0)
         load_dist(3, 1)
-        acc_rows.append(load_acc(1))
+        acc_rows = [load_acc(0), load_acc(1)]
 
         pop_grouped, pop_codes, pop_scales = {}, {}, {}
         squares, rates, rate_grouped, rate_codes, rate_scales = {}, {}, {}, {}, {}
@@ -234,14 +233,10 @@ def tile_forster_like_energy_transfer_s4_kernel(
             for i in (2 * pair, 2 * pair + 1):
                 turn_rate(i, 0)
                 turn_rate(i, 1)
-            if pair == 1:
-                turn_decay()
-            for i in (2 * pair, 2 * pair + 1):
-                quantize_rate(i)
-                if pair > 0:
-                    gain(i - 2, 0, C)
 
-        shared = (0, 1, 3)
+        on_vector = {1: (0, 0), 2: (1, 0), 3: (2, 0), 4: (2, 1), 5: (3, 0)}
+        on_scalar = {2: (0, 1), 4: (1, 1), 6: (3, 1)}
+        quantized = {2: 0, 4: 1, 5: 2, 6: 3}
         for pair in range(PAIRS):
             for h in range(2):
                 n = 2 * pair + h
@@ -250,18 +245,32 @@ def tile_forster_like_energy_transfer_s4_kernel(
                 inner_products(2 * pair, 2 * h + 1)
                 multiply_dist(2 * pair, h)
                 inner_products(2 * pair + 1, 2 * h + 1)
-                if n - 1 in shared:
-                    interleave_pop(n - 1, nc.scalar.copy, C // 2, C)
+                if n in on_scalar:
+                    g, side = on_scalar[n]
+                    interleave_pop(g, nc.scalar.copy, side * C // 2, (side + 1) * C // 2)
                 multiply_dist(2 * pair + 1, h)
-                if 0 <= n - 1 < J_PASSES:
-                    quantize_pop(n - 1)
-                if n < J_PASSES:
-                    interleave_pop(n, nc.vector.tensor_copy, 0, C // 2 if n in shared else C)
+                if n in quantized:
+                    quantize_pop(quantized[n])
+                if n in on_vector:
+                    g, side = on_vector[n]
+                    interleave_pop(g, nc.vector.tensor_copy, side * C // 2, (side + 1) * C // 2)
                 if n == J_PASSES:
                     nc.vector.tensor_scalar_mul(out=decay_rows[0:M_TILES, :], in0=decay_raw[:], scalar1=-1.0)
-            if pair > 0:
+            if pair in (1, 2):
                 turn_pair(pair - 1)
-        turn_pair(PAIRS - 1)
-        gain(M_TILES - 2, 0, C)
+                if pair == 2:
+                    turn_decay()
+                quantize_rate(2 * pair - 2)
+                quantize_rate(2 * pair - 1)
+        for pair in (2, 3):
+            first = 4 * (pair - 2)
+            turn_pair(pair)
+            quantize_rate(2 * pair)
+            gain(first, 0, C)
+            quantize_rate(2 * pair + 1)
+            gain(first + 1, 0, C)
+            gain(first + 2, 0, C)
+            if pair == 2:
+                gain(first + 3, 0, C)
         gain(M_TILES - 1, 0, C // 2)
         gain(M_TILES - 1, C // 2, C // 2)

from contextlib import ExitStack

import concourse.mybir as mybir
from concourse.masks import make_identity

M, K, J, C = 1024, 1536, 2048, 512
FLOPS = 2 * M * K * J + 2 * M * J * C

F32 = mybir.dt.float32
BF16 = mybir.dt.bfloat16
I32 = mybir.dt.int32
U32 = mybir.dt.uint32
U8 = mybir.dt.uint8
FP4X4 = mybir.dt.float4_e2m1fn_x4
FP8X4 = mybir.dt.float8_e4m3fn_x4
ACT = mybir.ActivationFunctionType
ALU = mybir.AluOpType

P = 128
BANK = 512
K_PASSES = K // 512
J_PASSES = J // 512
M_TILES = M // P
PAIRS = M_TILES // 2
ALIGN = 64


def tile_forster_like_energy_transfer_s4_kernel(
    tc, u_words, u_scales, v_words, v_scales, dist, pop, acc, decay, out
):
    nc = tc.nc
    with ExitStack() as ctx:
        keep = ctx.enter_context(tc.tile_pool(name="keep", bufs=1))
        work = ctx.enter_context(tc.tile_pool(name="work", bufs=4))
        psum = ctx.enter_context(tc.psum_pool(name="psum", bufs=1))
        ctx.enter_context(tc.manual_schedule())

        def kept(shape, dtype, name):
            return keep.tile(shape, dtype, name=name, align_bytes=ALIGN)

        def bank(tag):
            return psum.tile([P, BANK], F32, name=tag, tag=tag)

        sum_banks_taken = []

        def sum_bank():
            sum_banks_taken.append(None)
            return bank("sums%d" % (len(sum_banks_taken) % 4))

        def load_codes(words, first, count, name):
            codes = kept([P, K_PASSES, 2 * count], U8, name)
            src = words.bitcast(I32).rearrange("g p w -> p g w")
            nc.sync.dma_start(out=codes[:].bitcast(I32), in_=src[:, :, first // 2 : (first + count) // 2])
            return codes

        def scale_plane(count, name):
            plane = kept([P, K_PASSES, count], U8, name)
            nc.vector.memset(plane[:].bitcast(I32), 0)
            return plane

        def load_scale_rows(plane, scales, first, rows):
            count = plane.shape[2]
            src = scales.bitcast(I32).rearrange("g (q r) w -> r q g w", r=4)
            for r in rows:
                nc.sync.dma_start(
                    out=plane[r:P:32].bitcast(I32), in_=src[r, :, :, first // 4 : (first + count) // 4]
                )

        def load_dist(pair, h):
            rows = kept([P, 2, J // 2], BF16, "dist%d_%d" % (pair, h))
            src = dist[2 * P * pair : 2 * P * (pair + 1), h * J // 2 : (h + 1) * J // 2]
            nc.sync.dma_start(out=rows[:], in_=src.rearrange("(s p) j -> p s j", p=P))
            dist_rows[pair, h] = rows

        def load_acc(half):
            rows = kept([P, M_TILES // 2, C], BF16, "acc%d" % half)
            src = acc[half * M // 2 : (half + 1) * M // 2, :]
            nc.sync.dma_start(out=rows[:], in_=src.rearrange("(i p) c -> p i c", p=P))
            return rows

        def load_pop(g):
            raw = kept([P, 4, C], BF16, "pop_raw%d" % g)
            nc.sync.dma_start(out=raw[:], in_=pop[512 * g : 512 * (g + 1), :].rearrange("(p t) c -> p t c", t=4))
            return raw

        m_pair = 2 * P
        u_plane = [scale_plane(m_pair, "us0")]
        v_plane = [scale_plane(J // 2, "vs0"), scale_plane(J // 2, "vs1")]
        u_plane.append(scale_plane(M - m_pair, "us1"))
        ident_bf = kept([P, P], BF16, "ident_bf")
        nc.vector.memset(ident_bf[:], 0.0)
        make_identity(nc, ident_bf[:], nomemset=True)
        ident = kept([P, P], F32, "ident")
        nc.scalar.activation(out=ident[:], in_=ident_bf[:], func=ACT.Square)
        decay_rows = kept([P, P], F32, "decay_rows")
        nc.vector.memset(decay_rows[:], 0.0)

        dist_rows = {}
        load_scale_rows(u_plane[0], u_scales, 0, (0, 1))
        v_codes = [load_codes(v_words, 0, BANK, "vc0")]
        u_codes = [load_codes(u_words, 0, m_pair, "uc0")]
        load_scale_rows(u_plane[0], u_scales, 0, (2, 3))
        load_scale_rows(v_plane[0], v_scales, 0, range(4))
        v_codes.append(load_codes(v_words, BANK, BANK, "vc1"))
        load_scale_rows(v_plane[1], v_scales, J // 2, range(4))
        v_codes.append(load_codes(v_words, 2 * BANK, BANK, "vc2"))
        v_codes.append(load_codes(v_words, 3 * BANK, BANK, "vc3"))
        load_dist(0, 0)
        u_codes.append(load_codes(u_words, m_pair, m_pair, "uc1"))
        load_scale_rows(u_plane[1], u_scales, m_pair, range(4))
        load_dist(0, 1)
        pop_raw = [load_pop(0)]
        load_dist(1, 0)
        u_codes.append(load_codes(u_words, 2 * m_pair, 2 * m_pair, "uc2"))
        load_dist(1, 1)
        pop_raw.append(load_pop(1))
        decay_raw = kept([M_TILES, P], BF16, "decay_raw")
        nc.sync.dma_start(out=decay_raw[:], in_=decay.rearrange("(i p) -> i p", p=P))
        load_dist(2, 0)
        pop_raw.append(load_pop(2))
        load_dist(2, 1)
        pop_raw.append(load_pop(3))
        load_dist(3, 0)
        load_dist(3, 1)
        acc_rows = [load_acc(0), load_acc(1)]

        pop_grouped, pop_codes, pop_scales = {}, {}, {}
        squares, rates, rate_grouped, rate_codes, rate_scales = {}, {}, {}, {}, {}
        neg_decay = kept([P, M_TILES], F32, "neg_decay")

        def interleave_pop(g, copy, c0, c1):
            if g not in pop_grouped:
                pop_grouped[g] = kept([P, C, 4], BF16, "pop_grouped%d" % g)
            copy(
                out=pop_grouped[g][:, c0:c1, :].rearrange("p (c i) t -> p c t i", i=4),
                in_=pop_raw[g][:, :, c0:c1].rearrange("p t (c i) -> p c t i", i=4),
            )

        def quantize_pop(g):
            pop_codes[g] = kept([P, C], U32, "pop_codes%d" % g)
            pop_scales[g] = kept([P, C], U8, "pop_scales%d" % g)
            nc.vector.quantize_mx(
                out=pop_codes[g][:].bitcast(FP8X4),
                scales=pop_scales[g][:],
                in_=pop_grouped[g][:].rearrange("p c t -> p (c t)"),
            )

        def inner_products(i, g):
            part = min(i // 2, 2)
            col = i * P - part * m_pair
            s_part = min(i // 2, 1)
            s_col = i * P - s_part * m_pair
            products = sum_bank()
            v_col = (g % 2) * BANK
            for k in range(K_PASSES):
                nc.tensor.matmul_mx(
                    out=products[:],
                    lhsT=u_codes[part][:, k, 2 * col : 2 * (col + P)].bitcast(FP4X4),
                    lhsT_scale=u_plane[s_part][:, k, s_col : s_col + P],
                    rhs=v_codes[g][:, k, :].bitcast(FP4X4),
                    rhs_scale=v_plane[g // 2][:, k, v_col : v_col + BANK],
                    start=(k == 0),
                    stop=(k == K_PASSES - 1),
                )
            if g % 2 == 0:
                squares[i, g // 2] = work.tile([P, 2, 2, 256], F32, name="square", bufs=8)
            nc.scalar.activation(
                out=squares[i, g // 2][:, :, g % 2, :].rearrange("p u (q e) -> p u q e", e=2),
                in_=products[:].rearrange("p (q u e) -> p u q e", u=2, e=2),
                func=ACT.Square,
            )

        def multiply_dist(i, h):
            rate = work.tile([P, 2, 256, 2], BF16, name="rate", bufs=8, align_bytes=ALIGN)
            nc.vector.tensor_tensor(
                out=rate[:],
                in0=squares[i, h][:].rearrange("p u g (q e) -> p u (g q) e", e=2),
                in1=dist_rows[i // 2, h][:, i % 2, :].rearrange("p (q u e) -> p u q e", u=2, e=2),
                op=ALU.mult,
            )
            rates[i, h] = rate

        def turn_rate(i, h):
            words = rates[i, h][:].rearrange("p u q e -> p (u q e)").bitcast(F32)
            turned = bank("turned%d" % (2 * (i % 2) + h))
            for g in range(2):
                for u in range(2):
                    src = 256 * u + P * g
                    dst = 256 * g + P * u
                    nc.tensor.transpose(turned[:, dst : dst + P], words[:, src : src + P], ident[:])
            if h == 0:
                rate_grouped[i] = work.tile([P, J], BF16, name="rate_grouped", align_bytes=ALIGN)
            nc.scalar.copy(
                out=rate_grouped[i][:, 1024 * h : 1024 * (h + 1)].bitcast(F32).rearrange("p (g m u) -> p g m u", g=2, u=2),
                in_=turned[:].rearrange("p (g u m) -> p g m u", g=2, u=2),
            )

        def quantize_rate(i):
            rate_codes[i] = kept([P, BANK], U32, "rate_codes%d" % i)
            rate_scales[i] = kept([P, BANK], U8, "rate_scales%d" % i)
            nc.vector.quantize_mx(out=rate_codes[i][:].bitcast(FP8X4), scales=rate_scales[i][:], in_=rate_grouped[i][:])

        def turn_decay():
            turned = sum_bank()
            nc.tensor.transpose(turned[:, 0:P], decay_rows[:], ident[:])
            nc.scalar.copy(out=neg_decay[:], in_=turned[:, 0:M_TILES])

        def gain(i, c0, width):
            sums = sum_bank()
            for g in range(J_PASSES):
                cols = slice(g * P, (g + 1) * P)
                nc.tensor.matmul_mx(
                    out=sums[:, 0:width],
                    lhsT=rate_codes[i][:, cols].bitcast(FP8X4),
                    lhsT_scale=rate_scales[i][:, cols],
                    rhs=pop_codes[g][:, c0 : c0 + width].bitcast(FP8X4),
                    rhs_scale=pop_scales[g][:, c0 : c0 + width],
                    start=(g == 0),
                    stop=(g == J_PASSES - 1),
                )
            result = kept([P, width], F32, "result%d_%d" % (i, c0))
            nc.vector.scalar_tensor_tensor(
                out=result[:],
                in0=acc_rows[i // 4][:, i % 4, c0 : c0 + width],
                scalar=neg_decay[:, i : i + 1],
                in1=sums[:, 0:width],
                op0=ALU.mult,
                op1=ALU.add,
            )
            nc.sync.dma_start(out=out[i * P : (i + 1) * P, c0 : c0 + width], in_=result[:])

        def turn_pair(pair):
            for i in (2 * pair, 2 * pair + 1):
                turn_rate(i, 0)
                turn_rate(i, 1)

        on_vector = {1: (0, 0), 2: (1, 0), 3: (2, 0), 4: (2, 1), 5: (3, 0)}
        on_scalar = {2: (0, 1), 4: (1, 1), 6: (3, 1)}
        quantized = {2: 0, 4: 1, 5: 2, 6: 3}
        for pair in range(PAIRS):
            for h in range(2):
                n = 2 * pair + h
                inner_products(2 * pair, 2 * h)
                inner_products(2 * pair + 1, 2 * h)
                inner_products(2 * pair, 2 * h + 1)
                multiply_dist(2 * pair, h)
                inner_products(2 * pair + 1, 2 * h + 1)
                if n in on_scalar:
                    g, side = on_scalar[n]
                    interleave_pop(g, nc.scalar.copy, side * C // 2, (side + 1) * C // 2)
                multiply_dist(2 * pair + 1, h)
                if n in quantized:
                    quantize_pop(quantized[n])
                if n in on_vector:
                    g, side = on_vector[n]
                    interleave_pop(g, nc.vector.tensor_copy, side * C // 2, (side + 1) * C // 2)
                if n == J_PASSES:
                    nc.vector.tensor_scalar_mul(out=decay_rows[0:M_TILES, :], in0=decay_raw[:], scalar1=-1.0)
            if pair in (1, 2):
                turn_pair(pair - 1)
                if pair == 2:
                    turn_decay()
                quantize_rate(2 * pair - 2)
                quantize_rate(2 * pair - 1)
        for pair in (2, 3):
            first = 4 * (pair - 2)
            turn_pair(pair)
            quantize_rate(2 * pair)
            gain(first, 0, C)
            quantize_rate(2 * pair + 1)
            gain(first + 1, 0, C)
            gain(first + 2, 0, C)
            if pair == 2:
                gain(first + 3, 0, C)
        gain(M_TILES - 1, 0, C // 2)
        gain(M_TILES - 1, C // 2, C // 2)
